import numpy as np
import ml_dtypes


def mxq(x, axis, fmt="e4m3"):
    dtype, down = {"e4m3": (ml_dtypes.float8_e4m3fn, 7), "e5m2": (ml_dtypes.float8_e5m2, 14)}[fmt]
    v = np.moveaxis(np.asarray(x, np.float32).astype(ml_dtypes.bfloat16).astype(np.float64), axis, -1)
    blocks = v.reshape(v.shape[:-1] + (-1, 32))
    amax = np.abs(blocks).max(-1, keepdims=True)
    byte = np.maximum(np.where(amax > 0, np.frexp(amax)[1] - 1 + 127, 0) - down, 1)
    scale = np.exp2(byte - 127.0)
    codes = (blocks / scale).astype(np.float32).astype(dtype).astype(np.float64)
    return np.moveaxis((codes * scale).reshape(v.shape), -1, axis)


WIDE = False


def mx_kscale(k):
    if not WIDE:
        return np.ones(k)
    levels = np.array([10, -10, 5, -5, 0])
    if k % 512:
        return np.exp2(np.random.permutation(np.resize(levels, k // 32))).repeat(32)
    a = np.empty((k // 512, 16))
    for p in range(k // 512):
        a[p, :8] = np.random.permutation(np.resize(levels, 8))
        for g in range(8):
            far = levels[np.abs(levels - a[p, g]) >= 10]
            a[p, g + 8] = far[np.random.randint(len(far))]
    return np.exp2(a.ravel()).repeat(32)


def f64(x):
    return np.asarray(x).astype(np.float64)


def striped(idx):
    return np.tile(idx.reshape(-1, 16).T, (8, 1)).astype(np.uint16)


def unstriped(offs):
    return offs[:16].T.reshape(-1).astype(np.int64)


def pack_weight(w):
    k, n = w.shape
    w = f64(np.asarray(w, np.float32).astype(ml_dtypes.bfloat16)).reshape(k // 32, 32, n)
    amax = np.abs(w).max(1)
    byte = np.clip(np.where(amax > 0, np.frexp(amax)[1] - 1 + 127 - 7, 1), 1, 254)
    scaled = (w * np.exp2(127.0 - byte)[:, None, :]).reshape(k, n).astype(np.float32)
    words = np.ascontiguousarray(scaled.reshape(k // 512, 128, 4, n).transpose(0, 1, 3, 2)).astype(ml_dtypes.float8_e4m3fn).view(np.uint8)
    return words, np.ascontiguousarray(byte.astype(np.uint8).reshape(k // 512, 16, n))


def unpack_weight(words, scales):
    g, p, n, _ = words.shape
    vals = np.ascontiguousarray(words).view(ml_dtypes.float8_e4m3fn).astype(np.float64) * np.repeat(np.exp2(scales.astype(np.float64) - 127.0), 8, axis=1)[..., None]
    return vals.transpose(0, 1, 3, 2).reshape(g * 512, n)


K, T, E, C, N = 2048, 512, 4, 256, 128


def by_expert(wq, xq):
    return np.concatenate([wq[e].T @ xq[:, e * C:(e + 1) * C] for e in range(E)], axis=1)


def setup_inputs():
    n = np.random.standard_normal
    s = mx_kscale(K)[:, None]
    first = np.random.permutation(np.repeat(np.arange(E), T // E))
    second = (first + 1 + np.random.permutation(np.repeat(np.arange(E - 1), -(-T // (E - 1)))[:T])) % E
    while np.bincount(second, minlength=E).max() != T // E:
        load = np.bincount(second, minlength=E); hi, lo = int(load.argmax()), int(load.argmin())
        t = np.flatnonzero((second == hi) & (first != lo))[0]; second[t] = lo
    slot_token = np.empty(E * C, np.int64); pos = np.empty((2, T), np.int64); fill = np.zeros(E, np.int64)
    place = np.stack([np.random.permutation(C) for _ in range(E)])
    for r, deal in enumerate((first, second)):
        for t in np.random.permutation(T):
            e = deal[t]; j = e * C + place[e, fill[e]]; fill[e] += 1; slot_token[j] = t; pos[r, t] = j
    g = np.random.uniform(0.2, 0.8, T)
    packed = [pack_weight(m) for m in n((E, K, N)) / np.sqrt(K) / s[None]]
    return {
        "xT": (n((K, T)) * s).astype(np.float32),
        "w_words": np.stack([m[0] for m in packed]),
        "w_scales": np.stack([m[1] for m in packed]),
        "gate": np.stack([np.tile(g, (N, 1)), np.tile(1.0 - g, (N, 1))]).astype(np.float32),
        "offs": striped(slot_token),
        "pos1": striped(pos[0]),
        "pos2": striped(pos[1]),
    }


def reference(xT, w_words, w_scales, gate, offs, pos1, pos2):
    idx = unstriped(offs)
    xq = mxq(f64(xT)[:, idx], 0, "e4m3")
    w = np.stack([unpack_weight(w_words[e], w_scales[e]) for e in range(E)])
    y = by_expert(w, xq)
    return f64(gate[0]) * y[:, unstriped(pos1)] + f64(gate[1]) * y[:, unstriped(pos2)]

@@ -1,0 +1,163 @@
+from contextlib import ExitStack
+
+import concourse.mybir as mybir
+
+K, T, E, C, N = 2048, 512, 4, 256, 128
+FLOPS = 2 * K * N * E * C
+
+F32 = mybir.dt.float32
+BF16 = mybir.dt.bfloat16
+I32 = mybir.dt.int32
+U32 = mybir.dt.uint32
+U16 = mybir.dt.uint16
+U8 = mybir.dt.uint8
+FP8X4 = mybir.dt.float8_e4m3fn_x4
+MULT = mybir.AluOpType.mult
+ADD = mybir.AluOpType.add
+
+P = 128
+PACK = 4
+PASSES = K // (P * PACK)
+SLOTS = E * C
+HALF = T // 2
+WINDOW = 1536
+BYTE_WINDOW = 768
+WS_AFTER = 3
+HOLD = [0,256,256]
+LAST_CUTS = [[0,512],[512,768],[768,1024]]
+BYTE_CUTS = [[0,512],[512,1024]]
+BYTES_FIRST = True
+
+
+def tile_routed_moe_kernel(tc, xT, w_words, w_scales, gate, offs, pos1, pos2, out):
+    nc = tc.nc
+    with ExitStack() as ctx:
+        lists = ctx.enter_context(tc.tile_pool(name="lists", bufs=1))
+        keep = ctx.enter_context(tc.tile_pool(name="keep", bufs=1))
+        psum = ctx.enter_context(tc.psum_pool(name="psum", bufs=1))
+
+        offs_t = lists.tile([P, SLOTS // 16], U16, name="offs_t")
+        pos1_t = lists.tile([P, T // 16], U16, name="pos1_t")
+        pos2_t = lists.tile([P, T // 16], U16, name="pos2_t")
+
+        grouped = [keep.tile([P, T, PACK], BF16, name="grouped%d" % a, align_bytes=64) for a in range(PASSES)]
+        codes = keep.tile([P, PASSES * T + WINDOW - T], I32, name="codes", align_bytes=64)
+        planes = keep.tile([P, BYTE_WINDOW], U8, name="planes", align_bytes=64)
+        ww = [keep.tile([P, 2 * PASSES, N], I32, name="ww%d" % h, align_bytes=64) for h in range(2)]
+        ws = keep.tile([P, E * PASSES, N], U8, name="ws", align_bytes=64)
+        g = keep.tile([P, 2, T], F32, name="g")
+        y = keep.tile([P, SLOTS], F32, name="y")
+        t1 = keep.tile([P, T], F32, name="t1")
+        t2 = [keep.tile([P, HALF], F32, name="t2_%d" % h) for h in range(2)]
+        o = [keep.tile([P, HALF], F32, name="o_%d" % h) for h in range(2)]
+        acc = [psum.tile([P, C], F32, name="acc%d" % e) for e in range(E)]
+
+        nc.gpsimd.memset(planes[:], 0)
+        nc.vector.memset(codes[:, PASSES * T:], 0)
+        nc.vector.memset(ws[:].bitcast(I32), 0)
+
+        x_view = xT.rearrange("(a p j) t -> a p j t", p=P, j=PACK)
+        s_view = w_scales.rearrange("e a (q r) n -> r q (e a) n", r=4)
+        w_view = w_words.rearrange("(h e) a p n r -> h p (e a) (n r)", h=2)
+        raw = []
+        for a in range(PASSES):
+            pieces = []
+            for h in range(2):
+                piece = keep.tile([P, PACK, HALF], F32, name="raw%d_%d" % (a, h))
+                nc.sync.dma_start(piece[:], x_view[a][:, :, h * HALF:(h + 1) * HALF])
+                pieces.append(piece)
+            raw.append(pieces)
+            if a == 0:
+                nc.sync.dma_start(offs_t[:], offs)
+            if a == WS_AFTER:
+                for r in range(4):
+                    nc.sync.dma_start(ws[r:P:32, :, :].bitcast(I32), s_view[r].bitcast(I32))
+        for h in range(2):
+            nc.sync.dma_start(ww[h][:], w_view[h].bitcast(I32))
+        nc.sync.dma_start(g[:], gate.rearrange("r n t -> n r t"))
+        nc.sync.dma_start(pos1_t[:], pos1)
+        nc.sync.dma_start(pos2_t[:], pos2)
+
+        def cast(engine, a, h):
+            src = raw[a][h][:].rearrange("p j (c i) -> p c j i", i=4)
+            dst = grouped[a][:, h * HALF:(h + 1) * HALF, :].rearrange("p (c i) j -> p c j i", i=4)
+            if engine == "v":
+                nc.vector.tensor_copy(out=dst, in_=src)
+            else:
+                nc.scalar.copy(out=dst, in_=src)
+
+        def block(a):
+            return (PASSES - 1 - a) * T
+
+        def quantise(a, lo=0, hi=T):
+            nc.vector.quantize_mx(
+                out=codes[:, block(a) + lo:block(a) + hi].bitcast(FP8X4),
+                scales=planes[4 * a:P, lo:hi],
+                in_=grouped[a][:, lo:hi, :].rearrange("p t j -> p (t j)"),
+            )
+
+        held = {}
+
+        def gather(kind, a, lo, hi):
+            part = offs_t[:, lo // 16:hi // 16]
+            if kind == "w":
+                dst = keep.tile([P, hi - lo], U32, name="gw%d_%d" % (a, lo), align_bytes=64)
+                nc.vector.tensor_copy(out=dst[:], in_=codes[:, block(a):block(a) + WINDOW].bitcast(U32).indirect(part))
+            else:
+                dst = keep.tile([P, hi - lo], U8, name="gb_%d" % lo, align_bytes=64)
+                nc.vector.tensor_copy(out=dst[:], in_=planes[:].indirect(part))
+            for e in range(lo // C, hi // C):
+                held[(kind, a, e)] = (dst, e * C - lo)
+
+        def multiply(e, a):
+            words, w0 = held[("w", a, e)]
+            marks, b0 = held[("b", 0, e)]
+            nc.tensor.matmul_mx(
+                out=acc[e][:],
+                lhsT=ww[e // 2][:, (e % 2) * PASSES + a, :].bitcast(FP8X4),
+                lhsT_scale=ws[:, e * PASSES + a, :],
+                rhs=words[:, w0:w0 + C].bitcast(FP8X4),
+                rhs_scale=marks[4 * a:P, b0:b0 + C],
+                start=(a == 0),
+                stop=(a == PASSES - 1),
+            )
+
+        cast("v", 0, 0)
+        quantise(0, 0, HALF)
+        cast("v", 0, 1)
+        quantise(0, HALF, T)
+        for a in range(1, PASSES):
+            for h in range(2):
+                cast("s", a, h)
+
+        for a in range(PASSES - 1):
+            gather("w", a, 0, SLOTS - HOLD[a])
+            quantise(a + 1)
+            if HOLD[a]:
+                gather("w", a, SLOTS - HOLD[a], SLOTS)
+        last = PASSES - 1
+        if BYTES_FIRST:
+            for lo, hi in BYTE_CUTS:
+                gather("b", 0, lo, hi)
+            for lo, hi in LAST_CUTS:
+                gather("w", last, lo, hi)
+        else:
+            for (lo, hi), (lo2, hi2) in zip(BYTE_CUTS, LAST_CUTS):
+                gather("b", 0, lo, hi)
+                gather("w", last, lo2, hi2)
+
+        for a in range(PASSES - 1):
+            for e in range(E):
+                multiply(e, a)
+        for e in range(E):
+            multiply(e, last)
+            nc.scalar.copy(out=y[:, e * C:(e + 1) * C], in_=acc[e][:])
+
+        nc.vector.tensor_tensor(out=t1[:], in0=y[:].indirect(pos1_t[:]), in1=g[:, 0, :], op=MULT)
+        for h in range(2):
+            nc.vector.tensor_tensor(
+                out=t2[h][:], in0=y[:].indirect(pos2_t[:, h * (HALF // 16):(h + 1) * (HALF // 16)]), in1=g[:, 1, h * HALF:(h + 1) * HALF], op=MULT
+            )
+        for h in range(2):
+            nc.vector.tensor_tensor(out=o[h][:], in0=t1[:, h * HALF:(h + 1) * HALF], in1=t2[h][:], op=ADD)
+            nc.sync.dma_start(out[:, h * HALF:(h + 1) * HALF], o[h][:])

@@ -27,6 +27,7 @@ HOLD = [0,256,256]
 LAST_CUTS = [[0,512],[512,768],[768,1024]]
 BYTE_CUTS = [[0,512],[512,1024]]
 BYTES_FIRST = True
+V_SHARE = 168
 
 
 def tile_routed_moe_kernel(tc, xT, w_words, w_scales, gate, offs, pos1, pos2, out):
@@ -78,9 +79,9 @@ def tile_routed_moe_kernel(tc, xT, w_words, w_scales, gate, offs, pos1, pos2, ou
         nc.sync.dma_start(pos1_t[:], pos1)
         nc.sync.dma_start(pos2_t[:], pos2)
 
-        def cast(engine, a, h):
-            src = raw[a][h][:].rearrange("p j (c i) -> p c j i", i=4)
-            dst = grouped[a][:, h * HALF:(h + 1) * HALF, :].rearrange("p (c i) j -> p c j i", i=4)
+        def cast(engine, a, h, lo=0, hi=HALF):
+            src = raw[a][h][:, :, lo:hi].rearrange("p j (c i) -> p c j i", i=4)
+            dst = grouped[a][:, h * HALF + lo:h * HALF + hi, :].rearrange("p (c i) j -> p c j i", i=4)
             if engine == "v":
                 nc.vector.tensor_copy(out=dst, in_=src)
             else:
@@ -122,10 +123,10 @@ def tile_routed_moe_kernel(tc, xT, w_words, w_scales, gate, offs, pos1, pos2, ou
                 stop=(a == PASSES - 1),
             )
 
-        cast("v", 0, 0)
-        quantise(0, 0, HALF)
-        cast("v", 0, 1)
-        quantise(0, HALF, T)
+        for h in range(2):
+            cast("v", 0, h, 0, V_SHARE)
+            cast("s", 0, h, V_SHARE, HALF)
+            quantise(0, h * HALF, (h + 1) * HALF)
         for a in range(1, PASSES):
             for h in range(2):
                 cast("s", a, h)

@@ -28,6 +28,7 @@ LAST_CUTS = [[0,512],[512,768],[768,1024]]
 BYTE_CUTS = [[0,512],[512,1024]]
 BYTES_FIRST = True
 V_SHARE = 168
+G_SHARE = 64
 
 
 def tile_routed_moe_kernel(tc, xT, w_words, w_scales, gate, offs, pos1, pos2, out):
@@ -84,6 +85,8 @@ def tile_routed_moe_kernel(tc, xT, w_words, w_scales, gate, offs, pos1, pos2, ou
             dst = grouped[a][:, h * HALF + lo:h * HALF + hi, :].rearrange("p (c i) j -> p c j i", i=4)
             if engine == "v":
                 nc.vector.tensor_copy(out=dst, in_=src)
+            elif engine == "g":
+                nc.gpsimd.tensor_copy(out=dst, in_=src)
             else:
                 nc.scalar.copy(out=dst, in_=src)
 
@@ -129,7 +132,8 @@ def tile_routed_moe_kernel(tc, xT, w_words, w_scales, gate, offs, pos1, pos2, ou
             quantise(0, h * HALF, (h + 1) * HALF)
         for a in range(1, PASSES):
             for h in range(2):
-                cast("s", a, h)
+                cast("s", a, h, 0, HALF - G_SHARE)
+                cast("g", a, h, HALF - G_SHARE, HALF)
 
         for a in range(PASSES - 1):
             gather("w", a, 0, SLOTS - HOLD[a])

@@ -28,7 +28,7 @@ LAST_CUTS = [[0,512],[512,768],[768,1024]]
 BYTE_CUTS = [[0,512],[512,1024]]
 BYTES_FIRST = True
 V_SHARE = 168
-G_SHARE = 64
+G_SHARE = 128
 
 
 def tile_routed_moe_kernel(tc, xT, w_words, w_scales, gate, offs, pos1, pos2, out):

from contextlib import ExitStack

import concourse.mybir as mybir

K, T, E, C, N = 2048, 512, 4, 256, 128
FLOPS = 2 * K * N * E * C

F32 = mybir.dt.float32
BF16 = mybir.dt.bfloat16
I32 = mybir.dt.int32
U32 = mybir.dt.uint32
U16 = mybir.dt.uint16
U8 = mybir.dt.uint8
FP8X4 = mybir.dt.float8_e4m3fn_x4
MULT = mybir.AluOpType.mult
ADD = mybir.AluOpType.add

P = 128
PACK = 4
PASSES = K // (P * PACK)
SLOTS = E * C
HALF = T // 2
WINDOW = 1536
BYTE_WINDOW = 768
WS_AFTER = 3
HOLD = [0,256,256]
LAST_CUTS = [[0,512],[512,768],[768,1024]]
BYTE_CUTS = [[0,512],[512,1024]]
BYTES_FIRST = True
V_SHARE = 168
G_SHARE = 128


def tile_routed_moe_kernel(tc, xT, w_words, w_scales, gate, offs, pos1, pos2, out):
    nc = tc.nc
    with ExitStack() as ctx:
        lists = ctx.enter_context(tc.tile_pool(name="lists", bufs=1))
        keep = ctx.enter_context(tc.tile_pool(name="keep", bufs=1))
        psum = ctx.enter_context(tc.psum_pool(name="psum", bufs=1))

        offs_t = lists.tile([P, SLOTS // 16], U16, name="offs_t")
        pos1_t = lists.tile([P, T // 16], U16, name="pos1_t")
        pos2_t = lists.tile([P, T // 16], U16, name="pos2_t")

        grouped = [keep.tile([P, T, PACK], BF16, name="grouped%d" % a, align_bytes=64) for a in range(PASSES)]
        codes = keep.tile([P, PASSES * T + WINDOW - T], I32, name="codes", align_bytes=64)
        planes = keep.tile([P, BYTE_WINDOW], U8, name="planes", align_bytes=64)
        ww = [keep.tile([P, 2 * PASSES, N], I32, name="ww%d" % h, align_bytes=64) for h in range(2)]
        ws = keep.tile([P, E * PASSES, N], U8, name="ws", align_bytes=64)
        g = keep.tile([P, 2, T], F32, name="g")
        y = keep.tile([P, SLOTS], F32, name="y")
        t1 = keep.tile([P, T], F32, name="t1")
        t2 = [keep.tile([P, HALF], F32, name="t2_%d" % h) for h in range(2)]
        o = [keep.tile([P, HALF], F32, name="o_%d" % h) for h in range(2)]
        acc = [psum.tile([P, C], F32, name="acc%d" % e) for e in range(E)]

        nc.gpsimd.memset(planes[:], 0)
        nc.vector.memset(codes[:, PASSES * T:], 0)
        nc.vector.memset(ws[:].bitcast(I32), 0)

        x_view = xT.rearrange("(a p j) t -> a p j t", p=P, j=PACK)
        s_view = w_scales.rearrange("e a (q r) n -> r q (e a) n", r=4)
        w_view = w_words.rearrange("(h e) a p n r -> h p (e a) (n r)", h=2)
        raw = []
        for a in range(PASSES):
            pieces = []
            for h in range(2):
                piece = keep.tile([P, PACK, HALF], F32, name="raw%d_%d" % (a, h))
                nc.sync.dma_start(piece[:], x_view[a][:, :, h * HALF:(h + 1) * HALF])
                pieces.append(piece)
            raw.append(pieces)
            if a == 0:
                nc.sync.dma_start(offs_t[:], offs)
            if a == WS_AFTER:
                for r in range(4):
                    nc.sync.dma_start(ws[r:P:32, :, :].bitcast(I32), s_view[r].bitcast(I32))
        for h in range(2):
            nc.sync.dma_start(ww[h][:], w_view[h].bitcast(I32))
        nc.sync.dma_start(g[:], gate.rearrange("r n t -> n r t"))
        nc.sync.dma_start(pos1_t[:], pos1)
        nc.sync.dma_start(pos2_t[:], pos2)

        def cast(engine, a, h, lo=0, hi=HALF):
            src = raw[a][h][:, :, lo:hi].rearrange("p j (c i) -> p c j i", i=4)
            dst = grouped[a][:, h * HALF + lo:h * HALF + hi, :].rearrange("p (c i) j -> p c j i", i=4)
            if engine == "v":
                nc.vector.tensor_copy(out=dst, in_=src)
            elif engine == "g":
                nc.gpsimd.tensor_copy(out=dst, in_=src)
            else:
                nc.scalar.copy(out=dst, in_=src)

        def block(a):
            return (PASSES - 1 - a) * T

        def quantise(a, lo=0, hi=T):
            nc.vector.quantize_mx(
                out=codes[:, block(a) + lo:block(a) + hi].bitcast(FP8X4),
                scales=planes[4 * a:P, lo:hi],
                in_=grouped[a][:, lo:hi, :].rearrange("p t j -> p (t j)"),
            )

        held = {}

        def gather(kind, a, lo, hi):
            part = offs_t[:, lo // 16:hi // 16]
            if kind == "w":
                dst = keep.tile([P, hi - lo], U32, name="gw%d_%d" % (a, lo), align_bytes=64)
                nc.vector.tensor_copy(out=dst[:], in_=codes[:, block(a):block(a) + WINDOW].bitcast(U32).indirect(part))
            else:
                dst = keep.tile([P, hi - lo], U8, name="gb_%d" % lo, align_bytes=64)
                nc.vector.tensor_copy(out=dst[:], in_=planes[:].indirect(part))
            for e in range(lo // C, hi // C):
                held[(kind, a, e)] = (dst, e * C - lo)

        def multiply(e, a):
            words, w0 = held[("w", a, e)]
            marks, b0 = held[("b", 0, e)]
            nc.tensor.matmul_mx(
                out=acc[e][:],
                lhsT=ww[e // 2][:, (e % 2) * PASSES + a, :].bitcast(FP8X4),
                lhsT_scale=ws[:, e * PASSES + a, :],
                rhs=words[:, w0:w0 + C].bitcast(FP8X4),
                rhs_scale=marks[4 * a:P, b0:b0 + C],
                start=(a == 0),
                stop=(a == PASSES - 1),
            )

        for h in range(2):
            cast("v", 0, h, 0, V_SHARE)
            cast("s", 0, h, V_SHARE, HALF)
            quantise(0, h * HALF, (h + 1) * HALF)
        for a in range(1, PASSES):
            for h in range(2):
                cast("s", a, h, 0, HALF - G_SHARE)
                cast("g", a, h, HALF - G_SHARE, HALF)

        for a in range(PASSES - 1):
            gather("w", a, 0, SLOTS - HOLD[a])
            quantise(a + 1)
            if HOLD[a]:
                gather("w", a, SLOTS - HOLD[a], SLOTS)
        last = PASSES - 1
        if BYTES_FIRST:
            for lo, hi in BYTE_CUTS:
                gather("b", 0, lo, hi)
            for lo, hi in LAST_CUTS:
                gather("w", last, lo, hi)
        else:
            for (lo, hi), (lo2, hi2) in zip(BYTE_CUTS, LAST_CUTS):
                gather("b", 0, lo, hi)
                gather("w", last, lo2, hi2)

        for a in range(PASSES - 1):
            for e in range(E):
                multiply(e, a)
        for e in range(E):
            multiply(e, last)
            nc.scalar.copy(out=y[:, e * C:(e + 1) * C], in_=acc[e][:])

        nc.vector.tensor_tensor(out=t1[:], in0=y[:].indirect(pos1_t[:]), in1=g[:, 0, :], op=MULT)
        for h in range(2):
            nc.vector.tensor_tensor(
                out=t2[h][:], in0=y[:].indirect(pos2_t[:, h * (HALF // 16):(h + 1) * (HALF // 16)]), in1=g[:, 1, h * HALF:(h + 1) * HALF], op=MULT
            )
        for h in range(2):
            nc.vector.tensor_tensor(out=o[h][:], in0=t1[:, h * HALF:(h + 1) * HALF], in1=t2[h][:], op=ADD)
            nc.sync.dma_start(out[:, h * HALF:(h + 1) * HALF], o[h][:])
